import numpy as np
import ml_dtypes


def mxq(x, axis, fmt="e4m3"):
    dtype, down = {"e4m3": (ml_dtypes.float8_e4m3fn, 7), "e5m2": (ml_dtypes.float8_e5m2, 14)}[fmt]
    v = np.moveaxis(np.asarray(x, np.float32).astype(ml_dtypes.bfloat16).astype(np.float64), axis, -1)
    blocks = v.reshape(v.shape[:-1] + (-1, 32))
    amax = np.abs(blocks).max(-1, keepdims=True)
    byte = np.maximum(np.where(amax > 0, np.frexp(amax)[1] - 1 + 127, 0) - down, 1)
    scale = np.exp2(byte - 127.0)
    codes = (blocks / scale).astype(np.float32).astype(dtype).astype(np.float64)
    return np.moveaxis((codes * scale).reshape(v.shape), -1, axis)


WIDE = False


def mx_kscale(k):
    if not WIDE:
        return np.ones(k)
    levels = np.array([10, -10, 5, -5, 0])
    if k % 512:
        return np.exp2(np.random.permutation(np.resize(levels, k // 32))).repeat(32)
    a = np.empty((k // 512, 16))
    for p in range(k // 512):
        a[p, :8] = np.random.permutation(np.resize(levels, 8))
        for g in range(8):
            far = levels[np.abs(levels - a[p, g]) >= 10]
            a[p, g + 8] = far[np.random.randint(len(far))]
    return np.exp2(a.ravel()).repeat(32)


def f64(x):
    return np.asarray(x).astype(np.float64)


def striped(idx):
    return np.tile(idx.reshape(-1, 16).T, (8, 1)).astype(np.uint16)


def unstriped(offs):
    return offs[:16].T.reshape(-1).astype(np.int64)


def striped8(idx):
    return np.concatenate([x.reshape(-1, 16).T for x in idx]).astype(np.uint16)


def runs(offs, k):
    lists = np.stack([offs[16 * r : 16 * r + 16].T.reshape(-1) for r in range(8)]).astype(np.int64)
    return lists[np.arange(k) % 512 // 64]


def pack_weight(w):
    k, n = w.shape
    w = f64(np.asarray(w, np.float32).astype(ml_dtypes.bfloat16)).reshape(k // 32, 32, n)
    amax = np.abs(w).max(1)
    byte = np.clip(np.where(amax > 0, np.frexp(amax)[1] - 1 + 127 - 7, 1), 1, 254)
    scaled = (w * np.exp2(127.0 - byte)[:, None, :]).reshape(k, n).astype(np.float32)
    words = np.ascontiguousarray(scaled.reshape(k // 512, 128, 4, n).transpose(0, 1, 3, 2)).astype(ml_dtypes.float8_e4m3fn).view(np.uint8)
    return words, np.ascontiguousarray(byte.astype(np.uint8).reshape(k // 512, 16, n))


def unpack_weight(words, scales):
    g, p, n, _ = words.shape
    vals = np.ascontiguousarray(words).view(ml_dtypes.float8_e4m3fn).astype(np.float64) * np.repeat(np.exp2(scales.astype(np.float64) - 127.0), 8, axis=1)[..., None]
    return vals.transpose(0, 1, 3, 2).reshape(g * 512, n)


def sigmoid(v):
    return 1.0 / (1.0 + np.exp(-np.maximum(v, -700.0)))

def planes(y):
    n, m = y.shape
    v = y.astype(np.float32).astype(ml_dtypes.bfloat16).astype(np.float64).reshape(n // 32, 32, m)
    top = np.abs(v).max(1)
    byte = np.clip(np.where(top > 0, np.frexp(top)[1] - 1 + 127 - 7, 1), 1, 254)
    codes = (v * np.exp2(127.0 - byte)[:, None, :]).reshape(n, m).astype(np.float32).astype(ml_dtypes.float8_e4m3fn).view(np.uint8)
    words = codes.reshape(n // 512, 128, 4, m).transpose(0, 1, 3, 2)
    return np.ascontiguousarray(words), np.ascontiguousarray(byte.astype(np.uint8).reshape(n // 512, 16, m))


K, T, S, N, G, H = 512, 2048, 256, 512, 2048, 512


def setup_inputs():
    n = np.random.standard_normal
    s = mx_kscale(K)[:, None]
    u = mx_kscale(K)
    packed_xT = pack_weight(n((K, T)) * s)
    packed_dT = pack_weight(n((K, G)) / s)
    packed_w1 = pack_weight(n((H, N)) / np.sqrt(2 * H) / u[:, None])
    packed_w2 = pack_weight(n((K, N)) / np.sqrt(2 * K) / s)
    return {
        "x_words": packed_xT[0],
        "x_scales": packed_xT[1],
        "d_words": packed_dT[0],
        "d_scales": packed_dT[1],
        "gn": (np.random.uniform(0.5, 1.5, (H, 1)) * u[:, None]).astype(np.float32),
        "w1_words": packed_w1[0],
        "w1_scales": packed_w1[1],
        "w2_words": packed_w2[0],
        "w2_scales": packed_w2[1],
        "offs": striped(np.random.permutation(T)[:S]),
        "k1": striped8(np.random.randint(0, G, (8, H))),
        "n1": striped8(np.stack([np.random.permutation(S) for _ in range(8)])),
        "n2": striped8(np.stack([np.random.permutation(S) for _ in range(8)])),
        "two": striped(np.random.permutation(T)[:S]),
        "n3": striped8(np.stack([np.random.permutation(S) for _ in range(8)])),
        "n4": striped8(np.stack([np.random.permutation(S) for _ in range(8)])),
    }


def reference(x_words, x_scales, d_words, d_scales, gn, w1_words, w1_scales, w2_words, w2_scales, offs, k1, n1, n2, two, n3, n4):
    d_k1 = unpack_weight(d_words, d_scales)[np.arange(K)[:, None], runs(k1, K)]
    xq = unpack_weight(x_words, x_scales)[:, unstriped(offs)]
    s = 0.0625 * (d_k1.T @ xq)
    pa = s[np.arange(H)[:, None], runs(n1, H)]
    pb = s[np.arange(H)[:, None], runs(n2, H)]
    z = f64(gn) * (np.maximum(np.maximum(s, pa), pb) - (0.5 * (np.minimum(np.minimum(s, pa), pb))))
    x_two = unpack_weight(x_words, x_scales)[:, unstriped(two)]
    h = unpack_weight(w1_words, w1_scales).T @ mxq(z, 0, "e4m3") + unpack_weight(w2_words, w2_scales).T @ x_two
    out_0 = h + (sigmoid(h[np.arange(N)[:, None], runs(n3, N)])) * (h[np.arange(N)[:, None], runs(n4, N)] - h)
    return (out_0,) + planes(out_0)

@@ -1,0 +1,212 @@
+from contextlib import ExitStack
+
+import concourse.mybir as mybir
+
+K, T, S, N, G, H = 512, 2048, 256, 512, 2048, 512
+FLOPS = 2 * K * H * S + 2 * H * N * S + 2 * K * N * S
+
+F32 = mybir.dt.float32
+BF16 = mybir.dt.bfloat16
+I32 = mybir.dt.int32
+U32 = mybir.dt.uint32
+U16 = mybir.dt.uint16
+U8 = mybir.dt.uint8
+FP8X4 = mybir.dt.float8_e4m3fn_x4
+ALU = mybir.AluOpType
+ACT = mybir.ActivationFunctionType
+
+P = 128
+PACK = 4
+QUADS = 4
+WINDOW = 2 * S
+
+
+def tile_picked_kmixrangetrack_none_po_kernel(
+    tc, x_words, x_scales, d_words, d_scales, gn, w1_words, w1_scales, w2_words, w2_scales,
+    offs, k1, n1, n2, two, n3, n4, out_0, out_1, out_2,
+):
+    nc = tc.nc
+
+    def words_of(dram):
+        return dram[0].rearrange("p n t -> p (n t)").bitcast(I32)
+
+    def dealt(ap):
+        return ap.rearrange("p (t m) -> p m t", t=PACK)
+
+    def natural(ap):
+        return ap.rearrange("p (m t) -> p m t", t=PACK)
+
+    with ExitStack() as ctx:
+        lists = ctx.enter_context(tc.tile_pool(name="lists", bufs=1))
+        sb = ctx.enter_context(tc.tile_pool(name="sb", bufs=1))
+        psum = ctx.enter_context(tc.psum_pool(name="psum", bufs=1))
+
+        def load_list(name, dram):
+            tile = lists.tile([P, dram.shape[1]], U16, name=name)
+            nc.sync.dma_start(tile[:], dram)
+            return tile
+
+        def new(name, shape, dtype):
+            return sb.tile(shape, dtype, name=name, align_bytes=64)
+
+        d_table = new("d_table", [P, G], I32)
+        x_table = new("x_table", [P, T], I32)
+        d_rows = new("d_rows", [P, G], U8)
+        x_rows = new("x_rows", [P, T], U8)
+        d_plane = new("d_plane", [P, H], U8)
+        w_rows = new("w_rows", [P, N], U8)
+        windows = [new("window%d" % t, [P, WINDOW], F32) for t in range(PACK)]
+
+        nc.vector.memset(d_rows[:].bitcast(I32), 0)
+        nc.vector.memset(x_rows[:].bitcast(I32), 0)
+        nc.gpsimd.memset(d_plane[:].bitcast(I32), 0)
+        nc.gpsimd.memset(w_rows[:].bitcast(I32), 0)
+        for t in range(PACK):
+            nc.gpsimd.memset(windows[t][:, S:], 0.0)
+
+        k1_list = load_list("k1_list", k1)
+        nc.scalar.dma_start(d_table[:], words_of(d_words))
+        nc.scalar.dma_start(x_table[:], words_of(x_words))
+        nc.sync.dma_start(d_rows[0:P:8, :].bitcast(I32), d_scales[0].bitcast(I32))
+        for q in range(QUADS):
+            nc.sync.dma_start(
+                x_rows[32 * q : 32 * q + 4, :].bitcast(I32), x_scales[0, 4 * q : 4 * q + 4, :].bitcast(I32)
+            )
+        offs_list = load_list("offs_list", offs)
+        n1_list = load_list("n1_list", n1)
+        w2_raw = new("w2_raw", [P, N], I32)
+        nc.scalar.dma_start(w2_raw[:], words_of(w2_words))
+
+        d_picked_rows = new("d_picked_rows", [P, H], U8)
+        nc.vector.tensor_copy(d_picked_rows[:], d_rows[:].indirect(k1_list[:]))
+        d_dealt_rows = new("d_dealt_rows", [P, H], U8)
+        nc.vector.tensor_copy(dealt(d_dealt_rows[:]), natural(d_picked_rows[:]))
+        for q in range(QUADS):
+            nc.sync.dma_start(
+                d_plane[32 * q : 32 * q + 4, :].bitcast(I32),
+                d_dealt_rows[32 * q : 32 * q + 32 : 8, :].bitcast(I32),
+            )
+        n2_list = load_list("n2_list", n2)
+        two_list = load_list("two_list", two)
+        gain = new("gain", [P, PACK], F32)
+        nc.sync.dma_start(gain[:], gn.rearrange("(p t) o -> p (t o)", t=PACK))
+        w1_raw = new("w1_raw", [P, N], I32)
+        nc.sync.dma_start(w1_raw[:], words_of(w1_words))
+        for q in range(QUADS):
+            nc.sync.dma_start(
+                w_rows[32 * q : 32 * q + 4, :].bitcast(I32), w1_scales[0, 4 * q : 4 * q + 4, :].bitcast(I32)
+            )
+            nc.sync.dma_start(
+                w_rows[32 * q + 4 : 32 * q + 8, :].bitcast(I32), w2_scales[0, 4 * q : 4 * q + 4, :].bitcast(I32)
+            )
+        n3_list = load_list("n3_list", n3)
+        n4_list = load_list("n4_list", n4)
+
+        xq_plane = new("xq_plane", [P, S], U8)
+        nc.vector.tensor_copy(xq_plane[:], x_rows[:].indirect(offs_list[:]))
+        d_picked = new("d_picked", [P, H], U32)
+        nc.vector.tensor_copy(d_picked[:], d_table[:].bitcast(U32).indirect(k1_list[:]))
+        d_codes = new("d_codes", [P, H], U32)
+        nc.vector.tensor_copy(dealt(d_codes[:]), natural(d_picked[:]))
+        xq_codes = new("xq_codes", [P, S], U32)
+        nc.vector.tensor_copy(xq_codes[:], x_table[:].bitcast(U32).indirect(offs_list[:]))
+
+        s_banks = [psum.tile([P, S], F32, name="s_bank%d" % t) for t in range(PACK)]
+        for t in range(PACK):
+            cols = slice(P * t, P * (t + 1))
+            nc.tensor.matmul_mx(
+                out=s_banks[t][:], lhsT=d_codes[:, cols].bitcast(FP8X4), lhsT_scale=d_plane[:, cols],
+                rhs=xq_codes[:].bitcast(FP8X4), rhs_scale=xq_plane[:], start=True, stop=True,
+            )
+
+        x2_codes = new("x2_codes", [P, S], U32)
+        nc.vector.tensor_copy(x2_codes[:], x_table[:].bitcast(U32).indirect(two_list[:]))
+        x2_plane = new("x2_plane", [P, S], U8)
+        nc.vector.tensor_copy(x2_plane[:], x_rows[:].indirect(two_list[:]))
+        gain16 = new("gain16", [P, PACK], F32)
+        nc.vector.tensor_scalar(gain16[:], gain[:], 0.0625, None, ALU.mult)
+
+        w2_codes = new("w2_codes", [P, N], U32)
+        nc.gpsimd.tensor_copy(dealt(w2_codes[:]), natural(w2_raw[:].bitcast(U32)))
+        w1_codes = new("w1_codes", [P, N], U32)
+        nc.gpsimd.tensor_copy(dealt(w1_codes[:]), natural(w1_raw[:].bitcast(U32)))
+        w_planes = new("w_planes", [P, N], U8)
+        nc.gpsimd.tensor_copy(dealt(w_planes[:]), natural(w_rows[:]))
+
+        pa = new("pa", [P, PACK, S], F32)
+        pb = new("pb", [P, PACK, S], F32)
+        hi = new("hi", [P, PACK, S], F32)
+        lo = new("lo", [P, PACK, S], F32)
+        top = new("top", [P, PACK, S], F32)
+        low = new("low", [P, PACK, S], F32)
+        y = new("y", [P, PACK, S], F32)
+        z_bf = new("z_bf", [P, S, PACK], BF16)
+        for t in range(PACK):
+            nc.scalar.copy(windows[t][:, :S], s_banks[t][:])
+            nc.scalar.activation(pa[:, t, :], windows[t][:].indirect(n1_list[:]), ACT.Copy)
+            nc.scalar.activation(pb[:, t, :], windows[t][:].indirect(n2_list[:]), ACT.Copy)
+        for t in range(PACK):
+            nc.vector.tensor_tensor(hi[:, t, :], s_banks[t][:], pa[:, t, :], ALU.max)
+            nc.vector.tensor_tensor(lo[:, t, :], s_banks[t][:], pa[:, t, :], ALU.min)
+            nc.vector.tensor_tensor(top[:, t, :], hi[:, t, :], pb[:, t, :], ALU.max)
+            nc.vector.tensor_tensor(low[:, t, :], lo[:, t, :], pb[:, t, :], ALU.min)
+            nc.vector.scalar_tensor_tensor(y[:, t, :], low[:, t, :], -0.5, top[:, t, :], ALU.mult, ALU.add)
+            if t < 2:
+                nc.scalar.activation(z_bf[:, :, t], y[:, t, :], ACT.Copy, scale=gain16[:, t : t + 1])
+            else:
+                nc.vector.tensor_scalar(z_bf[:, :, t], y[:, t, :], gain16[:, t : t + 1], None, ALU.mult)
+        z_codes = new("z_codes", [P, S], U32)
+        z_plane = new("z_plane", [P, S], U8)
+        nc.vector.quantize_mx(
+            out=z_codes[:].bitcast(FP8X4), scales=z_plane[:], in_=z_bf[:].rearrange("p j t -> p (j t)")
+        )
+
+        h_banks = [psum.tile([P, S], F32, name="h_bank%d" % t) for t in range(PACK)]
+        for t in range(PACK):
+            cols = slice(P * t, P * (t + 1))
+            nc.tensor.matmul_mx(
+                out=h_banks[t][:], lhsT=w2_codes[:, cols].bitcast(FP8X4), lhsT_scale=w_planes[4:P, cols],
+                rhs=x2_codes[:].bitcast(FP8X4), rhs_scale=x2_plane[:], start=True, stop=False,
+            )
+        for t in range(PACK):
+            cols = slice(P * t, P * (t + 1))
+            nc.tensor.matmul_mx(
+                out=h_banks[t][:], lhsT=w1_codes[:, cols].bitcast(FP8X4), lhsT_scale=w_planes[:, cols],
+                rhs=z_codes[:].bitcast(FP8X4), rhs_scale=z_plane[:], start=False, stop=True,
+            )
+
+        gate = new("gate", [P, PACK, S], F32)
+        other = new("other", [P, PACK, S], F32)
+        diff = new("diff", [P, PACK, S], F32)
+        step = new("step", [P, PACK, S], F32)
+        result = new("result", [P, PACK, S], F32)
+        result_bf = new("result_bf", [P, S, PACK], BF16)
+        out_rows = out_0.rearrange("(p t) j -> p t j", t=PACK)
+        for t in range(PACK):
+            nc.vector.tensor_copy(windows[t][:, :S], h_banks[t][:])
+        for t in range(PACK):
+            if t == 0:
+                nc.scalar.activation(gate[:, t, :], windows[t][:].indirect(n3_list[:]), ACT.Sigmoid)
+            nc.scalar.activation(other[:, t, :], windows[t][:].indirect(n4_list[:]), ACT.Copy)
+            if t > 0:
+                nc.scalar.activation(gate[:, t, :], windows[t][:].indirect(n3_list[:]), ACT.Sigmoid)
+        for t in range(PACK):
+            nc.vector.tensor_tensor(diff[:, t, :], other[:, t, :], h_banks[t][:], ALU.subtract)
+            nc.vector.tensor_tensor(step[:, t, :], diff[:, t, :], gate[:, t, :], ALU.mult)
+            nc.vector.tensor_tensor(result[:, t, :], step[:, t, :], h_banks[t][:], ALU.add)
+            nc.sync.dma_start(out_rows[:, t, :], result[:, t, :])
+            if t < 2:
+                nc.scalar.copy(result_bf[:, :, t], result[:, t, :])
+            else:
+                nc.vector.tensor_copy(result_bf[:, :, t], result[:, t, :])
+        out_codes = new("out_codes", [P, S], I32)
+        out_plane = new("out_plane", [P, S], U8)
+        nc.vector.quantize_mx(
+            out=out_codes[:].bitcast(FP8X4), scales=out_plane[:], in_=result_bf[:].rearrange("p j t -> p (j t)")
+        )
+        nc.sync.dma_start(words_of(out_1), out_codes[:])
+        for q in range(QUADS):
+            queue = nc.scalar if q % 2 == 0 else nc.sync
+            queue.dma_start(
+                out_2[0, 4 * q : 4 * q + 4, :].bitcast(I32), out_plane[32 * q : 32 * q + 4, :].bitcast(I32)
+            )

@@ -46,52 +46,52 @@ def tile_picked_kmixrangetrack_none_po_kernel(
             nc.sync.dma_start(tile[:], dram)
             return tile
 
-        def new(name, shape, dtype):
-            return sb.tile(shape, dtype, name=name, align_bytes=64)
+        def new(name, shape, dtype, after=None):
+            return sb.tile(shape, dtype, name=name, tag=after or name, align_bytes=64)
 
         d_table = new("d_table", [P, G], I32)
         x_table = new("x_table", [P, T], I32)
         d_rows = new("d_rows", [P, G], U8)
         x_rows = new("x_rows", [P, T], U8)
         d_plane = new("d_plane", [P, H], U8)
-        w_rows = new("w_rows", [P, N], U8)
         windows = [new("window%d" % t, [P, WINDOW], F32) for t in range(PACK)]
 
-        nc.vector.memset(d_rows[:].bitcast(I32), 0)
+        nc.gpsimd.memset(d_rows[:].bitcast(I32), 0)
         nc.vector.memset(x_rows[:].bitcast(I32), 0)
-        nc.gpsimd.memset(d_plane[:].bitcast(I32), 0)
-        nc.gpsimd.memset(w_rows[:].bitcast(I32), 0)
+        nc.vector.memset(d_plane[:].bitcast(I32), 0)
         for t in range(PACK):
-            nc.gpsimd.memset(windows[t][:, S:], 0.0)
+            nc.vector.memset(windows[t][:, S:], 0.0)
 
         k1_list = load_list("k1_list", k1)
         nc.scalar.dma_start(d_table[:], words_of(d_words))
         nc.scalar.dma_start(x_table[:], words_of(x_words))
         nc.sync.dma_start(d_rows[0:P:8, :].bitcast(I32), d_scales[0].bitcast(I32))
         for q in range(QUADS):
-            nc.sync.dma_start(
+            nc.gpsimd.dma_start(
                 x_rows[32 * q : 32 * q + 4, :].bitcast(I32), x_scales[0, 4 * q : 4 * q + 4, :].bitcast(I32)
             )
         offs_list = load_list("offs_list", offs)
         n1_list = load_list("n1_list", n1)
+        n2_list = load_list("n2_list", n2)
+        two_list = load_list("two_list", two)
+        n3_list = load_list("n3_list", n3)
+        n4_list = load_list("n4_list", n4)
+        gain = new("gain", [P, PACK], F32)
+        nc.sync.dma_start(gain[:], gn.rearrange("(p t) o -> p (t o)", t=PACK))
         w2_raw = new("w2_raw", [P, N], I32)
-        nc.scalar.dma_start(w2_raw[:], words_of(w2_words))
+        nc.sync.dma_start(w2_raw[:], words_of(w2_words))
 
         d_picked_rows = new("d_picked_rows", [P, H], U8)
         nc.vector.tensor_copy(d_picked_rows[:], d_rows[:].indirect(k1_list[:]))
         d_dealt_rows = new("d_dealt_rows", [P, H], U8)
         nc.vector.tensor_copy(dealt(d_dealt_rows[:]), natural(d_picked_rows[:]))
         for q in range(QUADS):
-            nc.sync.dma_start(
+            nc.scalar.dma_start(
                 d_plane[32 * q : 32 * q + 4, :].bitcast(I32),
                 d_dealt_rows[32 * q : 32 * q + 32 : 8, :].bitcast(I32),
             )
-        n2_list = load_list("n2_list", n2)
-        two_list = load_list("two_list", two)
-        gain = new("gain", [P, PACK], F32)
-        nc.sync.dma_start(gain[:], gn.rearrange("(p t) o -> p (t o)", t=PACK))
-        w1_raw = new("w1_raw", [P, N], I32)
-        nc.sync.dma_start(w1_raw[:], words_of(w1_words))
+        w_rows = new("w_rows", [P, N], U8, after="d_dealt_rows")
+        nc.gpsimd.memset(w_rows[:].bitcast(I32), 0)
         for q in range(QUADS):
             nc.sync.dma_start(
                 w_rows[32 * q : 32 * q + 4, :].bitcast(I32), w1_scales[0, 4 * q : 4 * q + 4, :].bitcast(I32)
@@ -99,15 +99,15 @@ def tile_picked_kmixrangetrack_none_po_kernel(
             nc.sync.dma_start(
                 w_rows[32 * q + 4 : 32 * q + 8, :].bitcast(I32), w2_scales[0, 4 * q : 4 * q + 4, :].bitcast(I32)
             )
-        n3_list = load_list("n3_list", n3)
-        n4_list = load_list("n4_list", n4)
 
-        xq_plane = new("xq_plane", [P, S], U8)
-        nc.vector.tensor_copy(xq_plane[:], x_rows[:].indirect(offs_list[:]))
-        d_picked = new("d_picked", [P, H], U32)
+        d_picked = new("d_picked", [P, H], U32, after="d_picked_rows")
         nc.vector.tensor_copy(d_picked[:], d_table[:].bitcast(U32).indirect(k1_list[:]))
         d_codes = new("d_codes", [P, H], U32)
         nc.vector.tensor_copy(dealt(d_codes[:]), natural(d_picked[:]))
+        w1_raw = new("w1_raw", [P, N], I32, after="d_table")
+        nc.sync.dma_start(w1_raw[:], words_of(w1_words))
+        xq_plane = new("xq_plane", [P, S], U8)
+        nc.vector.tensor_copy(xq_plane[:], x_rows[:].indirect(offs_list[:]))
         xq_codes = new("xq_codes", [P, S], U32)
         nc.vector.tensor_copy(xq_codes[:], x_table[:].bitcast(U32).indirect(offs_list[:]))
 
@@ -119,22 +119,17 @@ def tile_picked_kmixrangetrack_none_po_kernel(
                 rhs=xq_codes[:].bitcast(FP8X4), rhs_scale=xq_plane[:], start=True, stop=True,
             )
 
-        x2_codes = new("x2_codes", [P, S], U32)
+        for t in range(PACK):
+            nc.vector.tensor_copy(windows[t][:, :S], s_banks[t][:])
+        x2_codes = new("x2_codes", [P, S], U32, after="xq_codes")
         nc.vector.tensor_copy(x2_codes[:], x_table[:].bitcast(U32).indirect(two_list[:]))
         x2_plane = new("x2_plane", [P, S], U8)
         nc.vector.tensor_copy(x2_plane[:], x_rows[:].indirect(two_list[:]))
         gain16 = new("gain16", [P, PACK], F32)
         nc.vector.tensor_scalar(gain16[:], gain[:], 0.0625, None, ALU.mult)
 
-        w2_codes = new("w2_codes", [P, N], U32)
-        nc.gpsimd.tensor_copy(dealt(w2_codes[:]), natural(w2_raw[:].bitcast(U32)))
-        w1_codes = new("w1_codes", [P, N], U32)
-        nc.gpsimd.tensor_copy(dealt(w1_codes[:]), natural(w1_raw[:].bitcast(U32)))
-        w_planes = new("w_planes", [P, N], U8)
-        nc.gpsimd.tensor_copy(dealt(w_planes[:]), natural(w_rows[:]))
-
-        pa = new("pa", [P, PACK, S], F32)
-        pb = new("pb", [P, PACK, S], F32)
+        pa = [new("pa%d" % t, [P, S], F32) for t in range(PACK)]
+        pb = [new("pb%d" % t, [P, S], F32) for t in range(PACK)]
         hi = new("hi", [P, PACK, S], F32)
         lo = new("lo", [P, PACK, S], F32)
         top = new("top", [P, PACK, S], F32)
@@ -142,19 +137,24 @@ def tile_picked_kmixrangetrack_none_po_kernel(
         y = new("y", [P, PACK, S], F32)
         z_bf = new("z_bf", [P, S, PACK], BF16)
         for t in range(PACK):
-            nc.scalar.copy(windows[t][:, :S], s_banks[t][:])
-            nc.scalar.activation(pa[:, t, :], windows[t][:].indirect(n1_list[:]), ACT.Copy)
-            nc.scalar.activation(pb[:, t, :], windows[t][:].indirect(n2_list[:]), ACT.Copy)
+            nc.scalar.activation(pa[t][:], windows[t][:].indirect(n1_list[:]), ACT.Copy)
+            nc.scalar.activation(pb[t][:], windows[t][:].indirect(n2_list[:]), ACT.Copy)
         for t in range(PACK):
-            nc.vector.tensor_tensor(hi[:, t, :], s_banks[t][:], pa[:, t, :], ALU.max)
-            nc.vector.tensor_tensor(lo[:, t, :], s_banks[t][:], pa[:, t, :], ALU.min)
-            nc.vector.tensor_tensor(top[:, t, :], hi[:, t, :], pb[:, t, :], ALU.max)
-            nc.vector.tensor_tensor(low[:, t, :], lo[:, t, :], pb[:, t, :], ALU.min)
+            nc.vector.tensor_tensor(hi[:, t, :], s_banks[t][:], pa[t][:], ALU.max)
+            nc.vector.tensor_tensor(lo[:, t, :], s_banks[t][:], pa[t][:], ALU.min)
+            nc.vector.tensor_tensor(top[:, t, :], hi[:, t, :], pb[t][:], ALU.max)
+            nc.vector.tensor_tensor(low[:, t, :], lo[:, t, :], pb[t][:], ALU.min)
             nc.vector.scalar_tensor_tensor(y[:, t, :], low[:, t, :], -0.5, top[:, t, :], ALU.mult, ALU.add)
             if t < 2:
                 nc.scalar.activation(z_bf[:, :, t], y[:, t, :], ACT.Copy, scale=gain16[:, t : t + 1])
             else:
                 nc.vector.tensor_scalar(z_bf[:, :, t], y[:, t, :], gain16[:, t : t + 1], None, ALU.mult)
+        w2_codes = new("w2_codes", [P, N], U32, after="pa0")
+        nc.scalar.copy(dealt(w2_codes[:]), natural(w2_raw[:].bitcast(U32)))
+        w1_codes = new("w1_codes", [P, N], U32, after="pa1")
+        nc.scalar.copy(dealt(w1_codes[:]), natural(w1_raw[:].bitcast(U32)))
+        w_planes = new("w_planes", [P, N], U8, after="pb1")
+        nc.vector.tensor_copy(dealt(w_planes[:]), natural(w_rows[:]))
         z_codes = new("z_codes", [P, S], U32)
         z_plane = new("z_plane", [P, S], U8)
         nc.vector.quantize_mx(
@@ -195,10 +195,7 @@ def tile_picked_kmixrangetrack_none_po_kernel(
             nc.vector.tensor_tensor(step[:, t, :], diff[:, t, :], gate[:, t, :], ALU.mult)
             nc.vector.tensor_tensor(result[:, t, :], step[:, t, :], h_banks[t][:], ALU.add)
             nc.sync.dma_start(out_rows[:, t, :], result[:, t, :])
-            if t < 2:
-                nc.scalar.copy(result_bf[:, :, t], result[:, t, :])
-            else:
-                nc.vector.tensor_copy(result_bf[:, :, t], result[:, t, :])
+            nc.vector.tensor_copy(result_bf[:, :, t], result[:, t, :])
         out_codes = new("out_codes", [P, S], I32)
         out_plane = new("out_plane", [P, S], U8)
         nc.vector.quantize_mx(

@@ -53,21 +53,20 @@ def tile_picked_kmixrangetrack_none_po_kernel(
         x_table = new("x_table", [P, T], I32)
         d_rows = new("d_rows", [P, G], U8)
         x_rows = new("x_rows", [P, T], U8)
-        d_plane = new("d_plane", [P, H], U8)
+        d_plane = new("d_plane", [P, H], U8, after="w2_raw")
         windows = [new("window%d" % t, [P, WINDOW], F32) for t in range(PACK)]
 
-        nc.gpsimd.memset(d_rows[:].bitcast(I32), 0)
+        nc.vector.memset(d_rows[:].bitcast(I32), 0)
         nc.vector.memset(x_rows[:].bitcast(I32), 0)
         nc.vector.memset(d_plane[:].bitcast(I32), 0)
-        for t in range(PACK):
-            nc.vector.memset(windows[t][:, S:], 0.0)
 
         k1_list = load_list("k1_list", k1)
-        nc.scalar.dma_start(d_table[:], words_of(d_words))
-        nc.scalar.dma_start(x_table[:], words_of(x_words))
+        nc.gpsimd.dma_start(d_table[:], words_of(d_words))
+        nc.gpsimd.memset(windows[0][:, S:], 0.0)
+        nc.gpsimd.dma_start(x_table[:], words_of(x_words))
         nc.sync.dma_start(d_rows[0:P:8, :].bitcast(I32), d_scales[0].bitcast(I32))
         for q in range(QUADS):
-            nc.gpsimd.dma_start(
+            nc.sync.dma_start(
                 x_rows[32 * q : 32 * q + 4, :].bitcast(I32), x_scales[0, 4 * q : 4 * q + 4, :].bitcast(I32)
             )
         offs_list = load_list("offs_list", offs)
@@ -77,20 +76,25 @@ def tile_picked_kmixrangetrack_none_po_kernel(
         n3_list = load_list("n3_list", n3)
         n4_list = load_list("n4_list", n4)
         gain = new("gain", [P, PACK], F32)
-        nc.sync.dma_start(gain[:], gn.rearrange("(p t) o -> p (t o)", t=PACK))
-        w2_raw = new("w2_raw", [P, N], I32)
-        nc.sync.dma_start(w2_raw[:], words_of(w2_words))
+        nc.gpsimd.dma_start(gain[:], gn.rearrange("(p t) o -> p (t o)", t=PACK))
+
+        for t in range(1, PACK):
+            nc.scalar.activation(windows[t][:, S:], windows[0][:, S:], ACT.Sigmoid)
 
         d_picked_rows = new("d_picked_rows", [P, H], U8)
         nc.vector.tensor_copy(d_picked_rows[:], d_rows[:].indirect(k1_list[:]))
         d_dealt_rows = new("d_dealt_rows", [P, H], U8)
         nc.vector.tensor_copy(dealt(d_dealt_rows[:]), natural(d_picked_rows[:]))
         for q in range(QUADS):
-            nc.scalar.dma_start(
+            nc.sync.dma_start(
                 d_plane[32 * q : 32 * q + 4, :].bitcast(I32),
                 d_dealt_rows[32 * q : 32 * q + 32 : 8, :].bitcast(I32),
             )
-        w_rows = new("w_rows", [P, N], U8, after="d_dealt_rows")
+        d_picked = new("d_picked", [P, H], U32, after="d_picked_rows")
+        nc.vector.tensor_copy(d_picked[:], d_table[:].bitcast(U32).indirect(k1_list[:]))
+        d_codes = new("d_codes", [P, H], U32)
+        nc.vector.tensor_copy(dealt(d_codes[:]), natural(d_picked[:]))
+        w_rows = new("w_rows", [P, N], U8, after="d_table")
         nc.gpsimd.memset(w_rows[:].bitcast(I32), 0)
         for q in range(QUADS):
             nc.sync.dma_start(
@@ -100,13 +104,7 @@ def tile_picked_kmixrangetrack_none_po_kernel(
                 w_rows[32 * q + 4 : 32 * q + 8, :].bitcast(I32), w2_scales[0, 4 * q : 4 * q + 4, :].bitcast(I32)
             )
 
-        d_picked = new("d_picked", [P, H], U32, after="d_picked_rows")
-        nc.vector.tensor_copy(d_picked[:], d_table[:].bitcast(U32).indirect(k1_list[:]))
-        d_codes = new("d_codes", [P, H], U32)
-        nc.vector.tensor_copy(dealt(d_codes[:]), natural(d_picked[:]))
-        w1_raw = new("w1_raw", [P, N], I32, after="d_table")
-        nc.sync.dma_start(w1_raw[:], words_of(w1_words))
-        xq_plane = new("xq_plane", [P, S], U8)
+        xq_plane = new("xq_plane", [P, S], U8, after="d_picked_rows")
         nc.vector.tensor_copy(xq_plane[:], x_rows[:].indirect(offs_list[:]))
         xq_codes = new("xq_codes", [P, S], U32)
         nc.vector.tensor_copy(xq_codes[:], x_table[:].bitcast(U32).indirect(offs_list[:]))
@@ -119,14 +117,19 @@ def tile_picked_kmixrangetrack_none_po_kernel(
                 rhs=xq_codes[:].bitcast(FP8X4), rhs_scale=xq_plane[:], start=True, stop=True,
             )
 
-        for t in range(PACK):
-            nc.vector.tensor_copy(windows[t][:, :S], s_banks[t][:])
-        x2_codes = new("x2_codes", [P, S], U32, after="xq_codes")
+        w2_raw = new("w2_raw", [P, N], I32, after="w2_raw")
+        nc.sync.dma_start(w2_raw[:], words_of(w2_words))
+        w1_raw = new("w1_raw", [P, N], I32, after="d_codes")
+        nc.sync.dma_start(w1_raw[:], words_of(w1_words))
+        x2_codes = new("x2_codes", [P, S], U32)
         nc.vector.tensor_copy(x2_codes[:], x_table[:].bitcast(U32).indirect(two_list[:]))
         x2_plane = new("x2_plane", [P, S], U8)
         nc.vector.tensor_copy(x2_plane[:], x_rows[:].indirect(two_list[:]))
         gain16 = new("gain16", [P, PACK], F32)
         nc.vector.tensor_scalar(gain16[:], gain[:], 0.0625, None, ALU.mult)
+
+        w_planes = new("w_planes", [P, N], U8)
+        nc.vector.tensor_copy(dealt(w_planes[:]), natural(w_rows[:]))
 
         pa = [new("pa%d" % t, [P, S], F32) for t in range(PACK)]
         pb = [new("pb%d" % t, [P, S], F32) for t in range(PACK)]
@@ -135,31 +138,56 @@ def tile_picked_kmixrangetrack_none_po_kernel(
         top = new("top", [P, PACK, S], F32)
         low = new("low", [P, PACK, S], F32)
         y = new("y", [P, PACK, S], F32)
-        z_bf = new("z_bf", [P, S, PACK], BF16)
+
+        def empty_scores(t):
+            nc.scalar.copy(windows[t][:, :S], s_banks[t][:])
+
+        empty_scores(0)
         for t in range(PACK):
             nc.scalar.activation(pa[t][:], windows[t][:].indirect(n1_list[:]), ACT.Copy)
+            if t + 1 < PACK:
+                empty_scores(t + 1)
             nc.scalar.activation(pb[t][:], windows[t][:].indirect(n2_list[:]), ACT.Copy)
+
+        whole = slice(0, S)
+        halves = [slice(0, S // 2), slice(S // 2, S)]
+
+        def combine(t, cols):
+            nc.vector.scalar_tensor_tensor(y[:, t, cols], low[:, t, cols], -0.5, top[:, t, cols], ALU.mult, ALU.add)
+
+        def finish_z(t, cols):
+            if t < 2:
+                nc.scalar.activation(z_bf[:, cols, t], y[:, t, cols], ACT.Copy, scale=gain16[:, t : t + 1])
+            else:
+                nc.vector.tensor_scalar(z_bf[:, cols, t], y[:, t, cols], gain16[:, t : t + 1], None, ALU.mult)
+
         for t in range(PACK):
             nc.vector.tensor_tensor(hi[:, t, :], s_banks[t][:], pa[t][:], ALU.max)
+            if t > 0:
+                combine(t - 1, whole)
             nc.vector.tensor_tensor(lo[:, t, :], s_banks[t][:], pa[t][:], ALU.min)
+            if t == 2:
+                w2_codes = new("w2_codes", [P, N], U32, after="pa2")
+                nc.scalar.copy(dealt(w2_codes[:]), natural(w2_raw[:].bitcast(U32)))
+                z_bf = new("z_bf", [P, S, PACK], BF16, after="w2_raw")
+                finish_z(0, whole)
+                finish_z(1, whole)
             nc.vector.tensor_tensor(top[:, t, :], hi[:, t, :], pb[t][:], ALU.max)
             nc.vector.tensor_tensor(low[:, t, :], lo[:, t, :], pb[t][:], ALU.min)
-            nc.vector.scalar_tensor_tensor(y[:, t, :], low[:, t, :], -0.5, top[:, t, :], ALU.mult, ALU.add)
-            if t < 2:
-                nc.scalar.activation(z_bf[:, :, t], y[:, t, :], ACT.Copy, scale=gain16[:, t : t + 1])
-            else:
-                nc.vector.tensor_scalar(z_bf[:, :, t], y[:, t, :], gain16[:, t : t + 1], None, ALU.mult)
-        w2_codes = new("w2_codes", [P, N], U32, after="pa0")
-        nc.scalar.copy(dealt(w2_codes[:]), natural(w2_raw[:].bitcast(U32)))
-        w1_codes = new("w1_codes", [P, N], U32, after="pa1")
+        w1_codes = new("w1_codes", [P, N], U32, after="pa3")
         nc.scalar.copy(dealt(w1_codes[:]), natural(w1_raw[:].bitcast(U32)))
-        w_planes = new("w_planes", [P, N], U8, after="pb1")
-        nc.vector.tensor_copy(dealt(w_planes[:]), natural(w_rows[:]))
+        finish_z(PACK - 2, whole)
+        for cols in halves:
+            combine(PACK - 1, cols)
+        for cols in halves:
+            finish_z(PACK - 1, cols)
         z_codes = new("z_codes", [P, S], U32)
         z_plane = new("z_plane", [P, S], U8)
-        nc.vector.quantize_mx(
-            out=z_codes[:].bitcast(FP8X4), scales=z_plane[:], in_=z_bf[:].rearrange("p j t -> p (j t)")
-        )
+        for cols in halves:
+            nc.vector.quantize_mx(
+                out=z_codes[:, cols].bitcast(FP8X4), scales=z_plane[:, cols],
+                in_=z_bf[:, cols, :].rearrange("p j t -> p (j t)"),
+            )
 
         h_banks = [psum.tile([P, S], F32, name="h_bank%d" % t) for t in range(PACK)]
         for t in range(PACK):
@@ -184,26 +212,47 @@ def tile_picked_kmixrangetrack_none_po_kernel(
         out_rows = out_0.rearrange("(p t) j -> p t j", t=PACK)
         for t in range(PACK):
             nc.vector.tensor_copy(windows[t][:, :S], h_banks[t][:])
-        for t in range(PACK):
-            if t == 0:
-                nc.scalar.activation(gate[:, t, :], windows[t][:].indirect(n3_list[:]), ACT.Sigmoid)
-            nc.scalar.activation(other[:, t, :], windows[t][:].indirect(n4_list[:]), ACT.Copy)
-            if t > 0:
-                nc.scalar.activation(gate[:, t, :], windows[t][:].indirect(n3_list[:]), ACT.Sigmoid)
-        for t in range(PACK):
-            nc.vector.tensor_tensor(diff[:, t, :], other[:, t, :], h_banks[t][:], ALU.subtract)
-            nc.vector.tensor_tensor(step[:, t, :], diff[:, t, :], gate[:, t, :], ALU.mult)
-            nc.vector.tensor_tensor(result[:, t, :], step[:, t, :], h_banks[t][:], ALU.add)
-            nc.sync.dma_start(out_rows[:, t, :], result[:, t, :])
-            nc.vector.tensor_copy(result_bf[:, :, t], result[:, t, :])
         out_codes = new("out_codes", [P, S], I32)
         out_plane = new("out_plane", [P, S], U8)
-        nc.vector.quantize_mx(
-            out=out_codes[:].bitcast(FP8X4), scales=out_plane[:], in_=result_bf[:].rearrange("p j t -> p (j t)")
-        )
-        nc.sync.dma_start(words_of(out_1), out_codes[:])
+        pieces = [(t, whole) for t in range(PACK - 1)] + [(PACK - 1, cols) for cols in halves]
+        for t, cols in pieces:
+            entries = slice(cols.start // 16, cols.stop // 16)
+            nc.scalar.activation(other[:, t, cols], windows[t][:].indirect(n4_list[:, entries]), ACT.Copy)
+            nc.scalar.activation(gate[:, t, cols], windows[t][:].indirect(n3_list[:, entries]), ACT.Sigmoid)
+
+        def subtract(t, cols):
+            nc.vector.tensor_tensor(diff[:, t, cols], other[:, t, cols], h_banks[t][:, cols], ALU.subtract)
+
+        def weigh(t, cols):
+            nc.vector.tensor_tensor(step[:, t, cols], diff[:, t, cols], gate[:, t, cols], ALU.mult)
+
+        def add_back(t, cols):
+            nc.vector.tensor_tensor(result[:, t, cols], step[:, t, cols], h_banks[t][:, cols], ALU.add)
+            nc.sync.dma_start(out_rows[:, t, cols], result[:, t, cols])
+
+        def round_result(copy, cols):
+            copy(result_bf[:, cols, :], result[:, :, cols].rearrange("p t j -> p j t"))
+
+        def quantise_result(cols):
+            nc.vector.quantize_mx(
+                out=out_codes[:, cols].bitcast(FP8X4), scales=out_plane[:, cols],
+                in_=result_bf[:, cols, :].rearrange("p j t -> p (j t)"),
+            )
+            nc.scalar.dma_start(words_of(out_1)[:, cols], out_codes[:, cols])
+
+        subtract(*pieces[0])
+        weigh(*pieces[0])
+        for before, piece in zip(pieces, pieces[1:]):
+            subtract(*piece)
+            add_back(*before)
+            weigh(*piece)
+        round_result(nc.scalar.copy, halves[0])
+        add_back(*pieces[-1])
+        round_result(nc.vector.tensor_copy, halves[1])
+        quantise_result(halves[0])
+        quantise_result(halves[1])
         for q in range(QUADS):
-            queue = nc.scalar if q % 2 == 0 else nc.sync
+            queue = nc.sync if q % 2 == 0 else nc.scalar
             queue.dma_start(
                 out_2[0, 4 * q : 4 * q + 4, :].bitcast(I32), out_plane[32 * q : 32 * q + 4, :].bitcast(I32)
             )

@@ -30,11 +30,11 @@ def tile_picked_kmixrangetrack_none_po_kernel(
     def words_of(dram):
         return dram[0].rearrange("p n t -> p (n t)").bitcast(I32)
 
-    def dealt(ap):
-        return ap.rearrange("p (t m) -> p m t", t=PACK)
-
-    def natural(ap):
-        return ap.rearrange("p (m t) -> p m t", t=PACK)
+    def deal(copy, out, in_, run):
+        copy(
+            out.rearrange("p (t c i) -> p c t i", t=PACK, i=run),
+            in_.rearrange("p (c i t) -> p c t i", t=PACK, i=run),
+        )
 
     with ExitStack() as ctx:
         lists = ctx.enter_context(tc.tile_pool(name="lists", bufs=1))
@@ -53,7 +53,7 @@ def tile_picked_kmixrangetrack_none_po_kernel(
         x_table = new("x_table", [P, T], I32)
         d_rows = new("d_rows", [P, G], U8)
         x_rows = new("x_rows", [P, T], U8)
-        d_plane = new("d_plane", [P, H], U8, after="w2_raw")
+        d_plane = new("d_plane", [P, H], U8)
         windows = [new("window%d" % t, [P, WINDOW], F32) for t in range(PACK)]
 
         nc.vector.memset(d_rows[:].bitcast(I32), 0)
@@ -77,6 +77,10 @@ def tile_picked_kmixrangetrack_none_po_kernel(
         n4_list = load_list("n4_list", n4)
         gain = new("gain", [P, PACK], F32)
         nc.gpsimd.dma_start(gain[:], gn.rearrange("(p t) o -> p (t o)", t=PACK))
+        w2_raw = new("w2_raw", [P, N], I32)
+        nc.gpsimd.dma_start(w2_raw[:], words_of(w2_words))
+        w2_codes = new("w2_codes", [P, N], U32)
+        deal(nc.scalar.copy, w2_codes[:], w2_raw[:].bitcast(U32), 4)
 
         for t in range(1, PACK):
             nc.scalar.activation(windows[t][:, S:], windows[0][:, S:], ACT.Sigmoid)
@@ -84,7 +88,7 @@ def tile_picked_kmixrangetrack_none_po_kernel(
         d_picked_rows = new("d_picked_rows", [P, H], U8)
         nc.vector.tensor_copy(d_picked_rows[:], d_rows[:].indirect(k1_list[:]))
         d_dealt_rows = new("d_dealt_rows", [P, H], U8)
-        nc.vector.tensor_copy(dealt(d_dealt_rows[:]), natural(d_picked_rows[:]))
+        deal(nc.vector.tensor_copy, d_dealt_rows[:], d_picked_rows[:], 16)
         for q in range(QUADS):
             nc.sync.dma_start(
                 d_plane[32 * q : 32 * q + 4, :].bitcast(I32),
@@ -93,9 +97,9 @@ def tile_picked_kmixrangetrack_none_po_kernel(
         d_picked = new("d_picked", [P, H], U32, after="d_picked_rows")
         nc.vector.tensor_copy(d_picked[:], d_table[:].bitcast(U32).indirect(k1_list[:]))
         d_codes = new("d_codes", [P, H], U32)
-        nc.vector.tensor_copy(dealt(d_codes[:]), natural(d_picked[:]))
+        deal(nc.vector.tensor_copy, d_codes[:], d_picked[:], 4)
         w_rows = new("w_rows", [P, N], U8, after="d_table")
-        nc.gpsimd.memset(w_rows[:].bitcast(I32), 0)
+        nc.vector.memset(w_rows[:].bitcast(I32), 0)
         for q in range(QUADS):
             nc.sync.dma_start(
                 w_rows[32 * q : 32 * q + 4, :].bitcast(I32), w1_scales[0, 4 * q : 4 * q + 4, :].bitcast(I32)
@@ -117,8 +121,6 @@ def tile_picked_kmixrangetrack_none_po_kernel(
                 rhs=xq_codes[:].bitcast(FP8X4), rhs_scale=xq_plane[:], start=True, stop=True,
             )
 
-        w2_raw = new("w2_raw", [P, N], I32, after="w2_raw")
-        nc.sync.dma_start(w2_raw[:], words_of(w2_words))
         w1_raw = new("w1_raw", [P, N], I32, after="d_codes")
         nc.sync.dma_start(w1_raw[:], words_of(w1_words))
         x2_codes = new("x2_codes", [P, S], U32)
@@ -128,9 +130,6 @@ def tile_picked_kmixrangetrack_none_po_kernel(
         gain16 = new("gain16", [P, PACK], F32)
         nc.vector.tensor_scalar(gain16[:], gain[:], 0.0625, None, ALU.mult)
 
-        w_planes = new("w_planes", [P, N], U8)
-        nc.vector.tensor_copy(dealt(w_planes[:]), natural(w_rows[:]))
-
         pa = [new("pa%d" % t, [P, S], F32) for t in range(PACK)]
         pb = [new("pb%d" % t, [P, S], F32) for t in range(PACK)]
         hi = new("hi", [P, PACK, S], F32)
@@ -138,6 +137,7 @@ def tile_picked_kmixrangetrack_none_po_kernel(
         top = new("top", [P, PACK, S], F32)
         low = new("low", [P, PACK, S], F32)
         y = new("y", [P, PACK, S], F32)
+        z_bf = new("z_bf", [P, S, PACK], BF16)
 
         def empty_scores(t):
             nc.scalar.copy(windows[t][:, :S], s_banks[t][:])
@@ -166,16 +166,15 @@ def tile_picked_kmixrangetrack_none_po_kernel(
             if t > 0:
                 combine(t - 1, whole)
             nc.vector.tensor_tensor(lo[:, t, :], s_banks[t][:], pa[t][:], ALU.min)
-            if t == 2:
-                w2_codes = new("w2_codes", [P, N], U32, after="pa2")
-                nc.scalar.copy(dealt(w2_codes[:]), natural(w2_raw[:].bitcast(U32)))
-                z_bf = new("z_bf", [P, S, PACK], BF16, after="w2_raw")
-                finish_z(0, whole)
-                finish_z(1, whole)
+            if t in (1, 2):
+                finish_z(t - 1, whole)
             nc.vector.tensor_tensor(top[:, t, :], hi[:, t, :], pb[t][:], ALU.max)
             nc.vector.tensor_tensor(low[:, t, :], lo[:, t, :], pb[t][:], ALU.min)
+            if t == 1:
+                w_planes = new("w_planes", [P, N], U8, after="pb1")
+                deal(nc.vector.tensor_copy, w_planes[:], w_rows[:], 16)
         w1_codes = new("w1_codes", [P, N], U32, after="pa3")
-        nc.scalar.copy(dealt(w1_codes[:]), natural(w1_raw[:].bitcast(U32)))
+        deal(nc.scalar.copy, w1_codes[:], w1_raw[:].bitcast(U32), 4)
         finish_z(PACK - 2, whole)
         for cols in halves:
             combine(PACK - 1, cols)

from contextlib import ExitStack

import concourse.mybir as mybir

K, T, S, N, G, H = 512, 2048, 256, 512, 2048, 512
FLOPS = 2 * K * H * S + 2 * H * N * S + 2 * K * N * S

F32 = mybir.dt.float32
BF16 = mybir.dt.bfloat16
I32 = mybir.dt.int32
U32 = mybir.dt.uint32
U16 = mybir.dt.uint16
U8 = mybir.dt.uint8
FP8X4 = mybir.dt.float8_e4m3fn_x4
ALU = mybir.AluOpType
ACT = mybir.ActivationFunctionType

P = 128
PACK = 4
QUADS = 4
WINDOW = 2 * S


def tile_picked_kmixrangetrack_none_po_kernel(
    tc, x_words, x_scales, d_words, d_scales, gn, w1_words, w1_scales, w2_words, w2_scales,
    offs, k1, n1, n2, two, n3, n4, out_0, out_1, out_2,
):
    nc = tc.nc

    def words_of(dram):
        return dram[0].rearrange("p n t -> p (n t)").bitcast(I32)

    def deal(copy, out, in_, run):
        copy(
            out.rearrange("p (t c i) -> p c t i", t=PACK, i=run),
            in_.rearrange("p (c i t) -> p c t i", t=PACK, i=run),
        )

    with ExitStack() as ctx:
        lists = ctx.enter_context(tc.tile_pool(name="lists", bufs=1))
        sb = ctx.enter_context(tc.tile_pool(name="sb", bufs=1))
        psum = ctx.enter_context(tc.psum_pool(name="psum", bufs=1))

        def load_list(name, dram):
            tile = lists.tile([P, dram.shape[1]], U16, name=name)
            nc.sync.dma_start(tile[:], dram)
            return tile

        def new(name, shape, dtype, after=None):
            return sb.tile(shape, dtype, name=name, tag=after or name, align_bytes=64)

        d_table = new("d_table", [P, G], I32)
        x_table = new("x_table", [P, T], I32)
        d_rows = new("d_rows", [P, G], U8)
        x_rows = new("x_rows", [P, T], U8)
        d_plane = new("d_plane", [P, H], U8)
        windows = [new("window%d" % t, [P, WINDOW], F32) for t in range(PACK)]

        nc.vector.memset(d_rows[:].bitcast(I32), 0)
        nc.vector.memset(x_rows[:].bitcast(I32), 0)
        nc.vector.memset(d_plane[:].bitcast(I32), 0)

        k1_list = load_list("k1_list", k1)
        nc.gpsimd.dma_start(d_table[:], words_of(d_words))
        nc.gpsimd.memset(windows[0][:, S:], 0.0)
        nc.gpsimd.dma_start(x_table[:], words_of(x_words))
        nc.sync.dma_start(d_rows[0:P:8, :].bitcast(I32), d_scales[0].bitcast(I32))
        for q in range(QUADS):
            nc.sync.dma_start(
                x_rows[32 * q : 32 * q + 4, :].bitcast(I32), x_scales[0, 4 * q : 4 * q + 4, :].bitcast(I32)
            )
        offs_list = load_list("offs_list", offs)
        n1_list = load_list("n1_list", n1)
        n2_list = load_list("n2_list", n2)
        two_list = load_list("two_list", two)
        n3_list = load_list("n3_list", n3)
        n4_list = load_list("n4_list", n4)
        gain = new("gain", [P, PACK], F32)
        nc.gpsimd.dma_start(gain[:], gn.rearrange("(p t) o -> p (t o)", t=PACK))
        w2_raw = new("w2_raw", [P, N], I32)
        nc.gpsimd.dma_start(w2_raw[:], words_of(w2_words))
        w2_codes = new("w2_codes", [P, N], U32)
        deal(nc.scalar.copy, w2_codes[:], w2_raw[:].bitcast(U32), 4)

        for t in range(1, PACK):
            nc.scalar.activation(windows[t][:, S:], windows[0][:, S:], ACT.Sigmoid)

        d_picked_rows = new("d_picked_rows", [P, H], U8)
        nc.vector.tensor_copy(d_picked_rows[:], d_rows[:].indirect(k1_list[:]))
        d_dealt_rows = new("d_dealt_rows", [P, H], U8)
        deal(nc.vector.tensor_copy, d_dealt_rows[:], d_picked_rows[:], 16)
        for q in range(QUADS):
            nc.sync.dma_start(
                d_plane[32 * q : 32 * q + 4, :].bitcast(I32),
                d_dealt_rows[32 * q : 32 * q + 32 : 8, :].bitcast(I32),
            )
        d_picked = new("d_picked", [P, H], U32, after="d_picked_rows")
        nc.vector.tensor_copy(d_picked[:], d_table[:].bitcast(U32).indirect(k1_list[:]))
        d_codes = new("d_codes", [P, H], U32)
        deal(nc.vector.tensor_copy, d_codes[:], d_picked[:], 4)
        w_rows = new("w_rows", [P, N], U8, after="d_table")
        nc.vector.memset(w_rows[:].bitcast(I32), 0)
        for q in range(QUADS):
            nc.sync.dma_start(
                w_rows[32 * q : 32 * q + 4, :].bitcast(I32), w1_scales[0, 4 * q : 4 * q + 4, :].bitcast(I32)
            )
            nc.sync.dma_start(
                w_rows[32 * q + 4 : 32 * q + 8, :].bitcast(I32), w2_scales[0, 4 * q : 4 * q + 4, :].bitcast(I32)
            )

        xq_plane = new("xq_plane", [P, S], U8, after="d_picked_rows")
        nc.vector.tensor_copy(xq_plane[:], x_rows[:].indirect(offs_list[:]))
        xq_codes = new("xq_codes", [P, S], U32)
        nc.vector.tensor_copy(xq_codes[:], x_table[:].bitcast(U32).indirect(offs_list[:]))

        s_banks = [psum.tile([P, S], F32, name="s_bank%d" % t) for t in range(PACK)]
        for t in range(PACK):
            cols = slice(P * t, P * (t + 1))
            nc.tensor.matmul_mx(
                out=s_banks[t][:], lhsT=d_codes[:, cols].bitcast(FP8X4), lhsT_scale=d_plane[:, cols],
                rhs=xq_codes[:].bitcast(FP8X4), rhs_scale=xq_plane[:], start=True, stop=True,
            )

        w1_raw = new("w1_raw", [P, N], I32, after="d_codes")
        nc.sync.dma_start(w1_raw[:], words_of(w1_words))
        x2_codes = new("x2_codes", [P, S], U32)
        nc.vector.tensor_copy(x2_codes[:], x_table[:].bitcast(U32).indirect(two_list[:]))
        x2_plane = new("x2_plane", [P, S], U8)
        nc.vector.tensor_copy(x2_plane[:], x_rows[:].indirect(two_list[:]))
        gain16 = new("gain16", [P, PACK], F32)
        nc.vector.tensor_scalar(gain16[:], gain[:], 0.0625, None, ALU.mult)

        pa = [new("pa%d" % t, [P, S], F32) for t in range(PACK)]
        pb = [new("pb%d" % t, [P, S], F32) for t in range(PACK)]
        hi = new("hi", [P, PACK, S], F32)
        lo = new("lo", [P, PACK, S], F32)
        top = new("top", [P, PACK, S], F32)
        low = new("low", [P, PACK, S], F32)
        y = new("y", [P, PACK, S], F32)
        z_bf = new("z_bf", [P, S, PACK], BF16)

        def empty_scores(t):
            nc.scalar.copy(windows[t][:, :S], s_banks[t][:])

        empty_scores(0)
        for t in range(PACK):
            nc.scalar.activation(pa[t][:], windows[t][:].indirect(n1_list[:]), ACT.Copy)
            if t + 1 < PACK:
                empty_scores(t + 1)
            nc.scalar.activation(pb[t][:], windows[t][:].indirect(n2_list[:]), ACT.Copy)

        whole = slice(0, S)
        halves = [slice(0, S // 2), slice(S // 2, S)]

        def combine(t, cols):
            nc.vector.scalar_tensor_tensor(y[:, t, cols], low[:, t, cols], -0.5, top[:, t, cols], ALU.mult, ALU.add)

        def finish_z(t, cols):
            if t < 2:
                nc.scalar.activation(z_bf[:, cols, t], y[:, t, cols], ACT.Copy, scale=gain16[:, t : t + 1])
            else:
                nc.vector.tensor_scalar(z_bf[:, cols, t], y[:, t, cols], gain16[:, t : t + 1], None, ALU.mult)

        for t in range(PACK):
            nc.vector.tensor_tensor(hi[:, t, :], s_banks[t][:], pa[t][:], ALU.max)
            if t > 0:
                combine(t - 1, whole)
            nc.vector.tensor_tensor(lo[:, t, :], s_banks[t][:], pa[t][:], ALU.min)
            if t in (1, 2):
                finish_z(t - 1, whole)
            nc.vector.tensor_tensor(top[:, t, :], hi[:, t, :], pb[t][:], ALU.max)
            nc.vector.tensor_tensor(low[:, t, :], lo[:, t, :], pb[t][:], ALU.min)
            if t == 1:
                w_planes = new("w_planes", [P, N], U8, after="pb1")
                deal(nc.vector.tensor_copy, w_planes[:], w_rows[:], 16)
        w1_codes = new("w1_codes", [P, N], U32, after="pa3")
        deal(nc.scalar.copy, w1_codes[:], w1_raw[:].bitcast(U32), 4)
        finish_z(PACK - 2, whole)
        for cols in halves:
            combine(PACK - 1, cols)
        for cols in halves:
            finish_z(PACK - 1, cols)
        z_codes = new("z_codes", [P, S], U32)
        z_plane = new("z_plane", [P, S], U8)
        for cols in halves:
            nc.vector.quantize_mx(
                out=z_codes[:, cols].bitcast(FP8X4), scales=z_plane[:, cols],
                in_=z_bf[:, cols, :].rearrange("p j t -> p (j t)"),
            )

        h_banks = [psum.tile([P, S], F32, name="h_bank%d" % t) for t in range(PACK)]
        for t in range(PACK):
            cols = slice(P * t, P * (t + 1))
            nc.tensor.matmul_mx(
                out=h_banks[t][:], lhsT=w2_codes[:, cols].bitcast(FP8X4), lhsT_scale=w_planes[4:P, cols],
                rhs=x2_codes[:].bitcast(FP8X4), rhs_scale=x2_plane[:], start=True, stop=False,
            )
        for t in range(PACK):
            cols = slice(P * t, P * (t + 1))
            nc.tensor.matmul_mx(
                out=h_banks[t][:], lhsT=w1_codes[:, cols].bitcast(FP8X4), lhsT_scale=w_planes[:, cols],
                rhs=z_codes[:].bitcast(FP8X4), rhs_scale=z_plane[:], start=False, stop=True,
            )

        gate = new("gate", [P, PACK, S], F32)
        other = new("other", [P, PACK, S], F32)
        diff = new("diff", [P, PACK, S], F32)
        step = new("step", [P, PACK, S], F32)
        result = new("result", [P, PACK, S], F32)
        result_bf = new("result_bf", [P, S, PACK], BF16)
        out_rows = out_0.rearrange("(p t) j -> p t j", t=PACK)
        for t in range(PACK):
            nc.vector.tensor_copy(windows[t][:, :S], h_banks[t][:])
        out_codes = new("out_codes", [P, S], I32)
        out_plane = new("out_plane", [P, S], U8)
        pieces = [(t, whole) for t in range(PACK - 1)] + [(PACK - 1, cols) for cols in halves]
        for t, cols in pieces:
            entries = slice(cols.start // 16, cols.stop // 16)
            nc.scalar.activation(other[:, t, cols], windows[t][:].indirect(n4_list[:, entries]), ACT.Copy)
            nc.scalar.activation(gate[:, t, cols], windows[t][:].indirect(n3_list[:, entries]), ACT.Sigmoid)

        def subtract(t, cols):
            nc.vector.tensor_tensor(diff[:, t, cols], other[:, t, cols], h_banks[t][:, cols], ALU.subtract)

        def weigh(t, cols):
            nc.vector.tensor_tensor(step[:, t, cols], diff[:, t, cols], gate[:, t, cols], ALU.mult)

        def add_back(t, cols):
            nc.vector.tensor_tensor(result[:, t, cols], step[:, t, cols], h_banks[t][:, cols], ALU.add)
            nc.sync.dma_start(out_rows[:, t, cols], result[:, t, cols])

        def round_result(copy, cols):
            copy(result_bf[:, cols, :], result[:, :, cols].rearrange("p t j -> p j t"))

        def quantise_result(cols):
            nc.vector.quantize_mx(
                out=out_codes[:, cols].bitcast(FP8X4), scales=out_plane[:, cols],
                in_=result_bf[:, cols, :].rearrange("p j t -> p (j t)"),
            )
            nc.scalar.dma_start(words_of(out_1)[:, cols], out_codes[:, cols])

        subtract(*pieces[0])
        weigh(*pieces[0])
        for before, piece in zip(pieces, pieces[1:]):
            subtract(*piece)
            add_back(*before)
            weigh(*piece)
        round_result(nc.scalar.copy, halves[0])
        add_back(*pieces[-1])
        round_result(nc.vector.tensor_copy, halves[1])
        quantise_result(halves[0])
        quantise_result(halves[1])
        for q in range(QUADS):
            queue = nc.sync if q % 2 == 0 else nc.scalar
            queue.dma_start(
                out_2[0, 4 * q : 4 * q + 4, :].bitcast(I32), out_plane[32 * q : 32 * q + 4, :].bitcast(I32)
            )
